import numpy as np
import ml_dtypes


def mxq(x, axis, fmt="e4m3"):
    dtype, down = {"e4m3": (ml_dtypes.float8_e4m3fn, 7), "e5m2": (ml_dtypes.float8_e5m2, 14)}[fmt]
    v = np.moveaxis(np.asarray(x, np.float32).astype(ml_dtypes.bfloat16).astype(np.float64), axis, -1)
    blocks = v.reshape(v.shape[:-1] + (-1, 32))
    amax = np.abs(blocks).max(-1, keepdims=True)
    byte = np.maximum(np.where(amax > 0, np.frexp(amax)[1] - 1 + 127, 0) - down, 1)
    scale = np.exp2(byte - 127.0)
    codes = (blocks / scale).astype(np.float32).astype(dtype).astype(np.float64)
    return np.moveaxis((codes * scale).reshape(v.shape), -1, axis)


WIDE = False


def mx_kscale(k):
    if not WIDE:
        return np.ones(k)
    levels = np.array([10, -10, 5, -5, 0])
    if k % 512:
        return np.exp2(np.random.permutation(np.resize(levels, k // 32))).repeat(32)
    a = np.empty((k // 512, 16))
    for p in range(k // 512):
        a[p, :8] = np.random.permutation(np.resize(levels, 8))
        for g in range(8):
            far = levels[np.abs(levels - a[p, g]) >= 10]
            a[p, g + 8] = far[np.random.randint(len(far))]
    return np.exp2(a.ravel()).repeat(32)


def f64(x):
    return np.asarray(x).astype(np.float64)


def striped(idx):
    return np.tile(idx.reshape(-1, 16).T, (8, 1)).astype(np.uint16)


def unstriped(offs):
    return offs[:16].T.reshape(-1).astype(np.int64)


E2M1 = np.array([0.0, 0.5, 1.0, 1.5, 2.0, 3.0, 4.0, 6.0, -0.0, -0.5, -1.0, -1.5, -2.0, -3.0, -4.0, -6.0])


def pack_weight(w, fmt):
    k, n = w.shape
    w = f64(np.asarray(w, np.float32).astype(ml_dtypes.bfloat16)).reshape(k // 32, 32, n)
    amax = np.abs(w).max(1)
    if fmt == "e4m3":
        byte = np.frexp(amax)[1] - 1 + 127 - 7
    else:
        mant, ex = np.frexp(amax / 6.0)
        byte = np.where(mant > 0.5, ex, ex - 1) + 127
    byte = np.clip(np.where(amax > 0, byte, 1), 1, 254)
    scaled = (w * np.exp2(127.0 - byte)[:, None, :]).reshape(k, n).astype(np.float32)
    by_word = np.ascontiguousarray(scaled.reshape(k // 512, 128, 4, n).transpose(0, 1, 3, 2))
    if fmt == "e4m3":
        words = by_word.astype(ml_dtypes.float8_e4m3fn).view(np.uint8)
    else:
        c = by_word.astype(ml_dtypes.float4_e2m1fn).view(np.uint8) & 0xF
        words = (c[..., 0::2] | (c[..., 1::2] << 4)).reshape(k // 512, 128, 2 * n)
    return np.ascontiguousarray(words), np.ascontiguousarray(byte.astype(np.uint8).reshape(k // 512, 16, n))


def unpack_weight(words, scales, fmt):
    g, _, n = scales.shape
    words = np.ascontiguousarray(words).reshape(g, 128, n, -1)
    if fmt == "e4m3":
        vals = words.view(ml_dtypes.float8_e4m3fn).astype(np.float64)
    else:
        nib = np.empty((g, 128, n, 4), np.uint8)
        nib[..., 0::2] = words & 0xF
        nib[..., 1::2] = words >> 4
        vals = E2M1[nib]
    vals = vals * np.repeat(np.exp2(scales.astype(np.float64) - 127.0), 8, axis=1)[..., None]
    return vals.transpose(0, 1, 3, 2).reshape(g * 512, n)


def gelu(v):
    return 0.5 * v * (1.0 + np.tanh(np.sqrt(2.0 / np.pi) * (v + 0.044715 * v**3)))


K, H, T, S, T2, P = 1536, 1024, 4096, 1024, 2048, 512

def setup_inputs():
    n = np.random.standard_normal
    s = mx_kscale(K)[:, None]
    u = mx_kscale(H)[:, None]
    d = {}
    d["tab_words"], d["tab_scales"] = pack_weight(n((K, T)) * s, "e4m3")
    d["offs"] = striped(np.random.permutation(T)[:S])
    d["w1_words"], d["w1_scales"] = pack_weight(1.6 * n((K, H)) / K**0.5 / s, "e2m1")
    d["gain"] = (1.4 * np.exp(0.3 * n(H)) * u[:, 0]).astype(np.float32)
    d["page0"] = (n((H, T2)) * u).astype(np.float32)
    d["wgs"] = np.exp(0.3 * n((128, S))).astype(np.float32)
    d["offs2"] = striped(np.random.permutation(T2)[:S])
    d["offs3"] = striped(np.random.permutation(T2)[:P])
    d["offs4"] = striped(np.random.permutation(T2)[:P])
    d["sc"] = (0.9 * np.exp(0.25 * n(H)) / np.sqrt(u[:, 0])).astype(np.float32)
    d["w2"] = (n((H, H)) / H**0.5 / u).astype(np.float32)
    d["tw"] = (1.2 * np.exp(0.3 * n(H)) / u[:, 0]).astype(np.float32)
    return d

def reference(tab_words, tab_scales, offs, w1_words, w1_scales, gain, page0, wgs, offs2, offs3, offs4, sc, w2, tw):
    v = unpack_weight(tab_words, tab_scales, "e4m3")[:, unstriped(offs)]
    w1 = unpack_weight(w1_words, w1_scales, "e2m1")
    h = np.tanh(w1.T @ v) * f64(gain)[:, None]
    page = f64(page0).copy()
    page[:, unstriped(offs2)] = np.tile(f64(wgs), (H // 128, 1)) * h
    x = np.square(page[:, unstriped(offs3)] * f64(sc)[:, None])
    y = mxq(f64(w2), 0, "e4m3").T @ mxq(x, 0, "e4m3")
    twin = page[:, unstriped(offs4)] * f64(tw)[:, None]
    return np.abs(y - twin)

@@ -1,0 +1,231 @@
+from contextlib import ExitStack
+
+import concourse.mybir as mybir
+
+K, H, T, S, T2, M = 1536, 1024, 4096, 1024, 2048, 512
+FLOPS = 2 * K * H * S + 2 * H * H * M
+
+F32 = mybir.dt.float32
+BF16 = mybir.dt.bfloat16
+I32 = mybir.dt.int32
+U32 = mybir.dt.uint32
+U16 = mybir.dt.uint16
+U8 = mybir.dt.uint8
+FP8X4 = mybir.dt.float8_e4m3fn_x4
+FP4X4 = mybir.dt.float4_e2m1fn_x4
+ACT = mybir.ActivationFunctionType
+ALU = mybir.AluOpType
+
+P = 128
+PACK = 4
+BANK = 512
+PASSES1 = K // (P * PACK)
+PASSES2 = H // (P * PACK)
+SLICES = H // P
+W1_EARLY = 2
+TWINS_EARLY = 6
+W2_CHUNK = 512
+AHEAD = 2
+
+
+def tile_list_die_wear_ledger_kernel(
+    tc, tab_words, tab_scales, offs, w1_words, w1_scales, gain, page0, wgs, offs2, offs3, offs4, sc, w2, tw, out
+):
+    nc = tc.nc
+    with ExitStack() as ctx:
+        lists = ctx.enter_context(tc.tile_pool(name="lists", bufs=1))
+        keep = ctx.enter_context(tc.tile_pool(name="keep", bufs=1))
+        psum = ctx.enter_context(tc.psum_pool(name="psum", bufs=8))
+
+        idx = lists.tile([P, S // 16], U16, name="idx")
+        idx2 = lists.tile([P, S // 16], U16, name="idx2")
+        idx3 = lists.tile([P, M // 16], U16, name="idx3")
+        idx4 = lists.tile([P, M // 16], U16, name="idx4")
+
+        tab_sc = keep.tile([P, T], U8, name="tab_sc", align_bytes=64)
+        v_plane = keep.tile([P, PASSES1, S], U8, name="v_plane", align_bytes=64)
+        w1_plane = keep.tile([P, PASSES1, H], U8, name="w1_plane", align_bytes=64)
+        nc.vector.memset(w1_plane[:].bitcast(I32), 0)
+        nc.vector.memset(tab_sc[0:16, :].bitcast(I32), 0)
+        nc.vector.memset(tab_sc[64:128, :].bitcast(I32), 0)
+        nc.vector.memset(v_plane[:].bitcast(I32), 0)
+
+        tab = [keep.tile([P, T], U32, name=f"tab{a}", tag=f"big{a}", align_bytes=64) for a in range(PASSES1)]
+
+        def load_tab(a):
+            nc.sync.dma_start(tab[a][:].bitcast(I32), tab_words[a].rearrange("p t i -> p (t i)").bitcast(I32))
+
+        def load_column_vector(queue, name, vec):
+            col = keep.tile([P, SLICES], F32, name=name)
+            with nc.allow_non_contiguous_dma(reason="one value a partition and slice"):
+                queue.dma_start(col[:], vec.rearrange("(s p) -> p s", p=P))
+            return col
+
+        w1_rows = w1_words.rearrange("a p c -> p a c")
+        early_bytes = 2 * P * W1_EARLY
+        w1_early = keep.tile([P, PASSES1, early_bytes], U8, name="w1_early", align_bytes=64)
+        w1_late = keep.tile([P, PASSES1, 2 * H - early_bytes], U8, name="w1_late", align_bytes=64)
+        wgs_sb = keep.tile([P, S], F32, name="wgs_sb")
+        page = [keep.tile([P, T2], F32, name=f"page{s}") for s in range(SLICES)]
+
+        def load_page(s):
+            nc.sync.dma_start(page[s][:], page0[s * P : (s + 1) * P, :])
+
+        nc.sync.dma_start(idx[:], offs)
+        nc.sync.dma_start(tab_sc[16:64, :].bitcast(I32), tab_scales.rearrange("a q t -> q a t").bitcast(I32))
+        load_tab(0)
+        for q in range(4):
+            nc.sync.dma_start(
+                w1_plane[32 * q : 32 * q + 4, :, :].bitcast(I32),
+                w1_scales[:, 4 * q : 4 * q + 4, :].rearrange("a r c -> r a c").bitcast(I32),
+            )
+        load_tab(1)
+        v_sc = keep.tile([P, S], U8, name="v_sc", align_bytes=64)
+        nc.vector.tensor_copy(v_sc[:], tab_sc[:].indirect(idx[:]))
+        for q in range(4):
+            nc.sync.dma_start(
+                v_plane[32 * q : 32 * q + 4, :, :].bitcast(I32), v_sc[16 + 12 * q : 28 + 12 * q, :].bitcast(I32)
+            )
+        gain_sb = load_column_vector(nc.scalar, "gain_sb", gain)
+        sc_sb = load_column_vector(nc.scalar, "sc_sb", sc)
+        nc.sync.dma_start(w1_early[:].bitcast(I32), w1_rows[:, :, 0:early_bytes].bitcast(I32))
+        nc.sync.dma_start(idx2[:], offs2)
+        load_tab(2)
+        nc.sync.dma_start(wgs_sb[:], wgs)
+        load_page(0)
+        nc.sync.dma_start(idx3[:], offs3)
+        load_page(1)
+        nc.sync.dma_start(w1_late[:].bitcast(I32), w1_rows[:, :, early_bytes : 2 * H].bitcast(I32))
+
+        v_words = [keep.tile([P, S], U32, name=f"v_words{a}", align_bytes=64) for a in range(PASSES1)]
+        for a in range(PASSES1 - 1):
+            nc.vector.tensor_copy(v_words[a][:], tab[a][:].indirect(idx[:]))
+        for half in range(2):
+            nc.vector.tensor_copy(
+                v_words[PASSES1 - 1][:, half * BANK : (half + 1) * BANK],
+                tab[PASSES1 - 1][:].indirect(idx[:, half * 32 : (half + 1) * 32]),
+            )
+
+        w2_raw = []
+        for b in range(PASSES2):
+            load_page(2 + b)
+            raw = keep.tile([P, PACK, H], F32, name=f"w2_raw{b}", tag=f"big{b + 1}", align_bytes=64)
+            nc.sync.dma_start(raw[:], w2[b * 512 : (b + 1) * 512, :].rearrange("(p j) n -> p j n", j=PACK))
+            w2_raw.append(raw)
+        for s in range(2 + PASSES2, SLICES):
+            load_page(s)
+        nc.sync.dma_start(idx4[:], offs4)
+        tw_sb = load_column_vector(nc.sync, "tw_sb", tw)
+
+        w2_codes = keep.tile([P, PASSES2, H], U32, name="w2_codes", align_bytes=64)
+        w2_plane = keep.tile([P, PASSES2, H], U8, name="w2_plane", align_bytes=64)
+
+        def quantise_w2(chunk):
+            b, c0 = divmod(chunk * W2_CHUNK, H)
+            grouped = keep.tile([P, W2_CHUNK * PACK], BF16, name="w2_grouped", bufs=2, align_bytes=64)
+            nc.scalar.copy(
+                grouped[:].rearrange("p (c i j) -> p c j i", i=4, j=PACK),
+                w2_raw[b][:, :, c0 : c0 + W2_CHUNK].rearrange("p j (c i) -> p c j i", i=4),
+            )
+            nc.vector.quantize_mx(
+                w2_codes[:, b, c0 : c0 + W2_CHUNK].bitcast(FP8X4), w2_plane[:, b, c0 : c0 + W2_CHUNK], grouped[:]
+            )
+
+        x_rows = [keep.tile([P, PACK, M], BF16, name=f"x_rows{b}") for b in range(PASSES2)]
+        x_codes = [keep.tile([P, M], U32, name=f"x_codes{b}", align_bytes=64) for b in range(PASSES2)]
+        x_plane = [keep.tile([P, M], U8, name=f"x_plane{b}", align_bytes=64) for b in range(PASSES2)]
+
+        def new_entries(s):
+            if s < W1_EARLY:
+                w1_sb, c0 = w1_early, 2 * P * s
+            else:
+                w1_sb, c0 = w1_late, 2 * P * (s - W1_EARLY)
+            if s == SLICES - 1:
+                h = keep.tile([P, S], F32, name="h_last", tag="big0", align_bytes=64)
+            else:
+                h = keep.tile([P, S], F32, name="h", bufs=3)
+            wg = keep.tile([P, S], F32, name="wg", bufs=3)
+            nc.scalar.activation(wg[:], wgs_sb[:], ACT.Copy, scale=gain_sb[:, s : s + 1])
+            for half in range(2):
+                cols = slice(half * BANK, (half + 1) * BANK)
+                acc = psum.tile([P, BANK], F32, name="bank")
+                for a in range(PASSES1):
+                    nc.tensor.matmul_mx(
+                        acc[:],
+                        lhsT=w1_sb[:, a, c0 : c0 + 2 * P].bitcast(FP4X4),
+                        lhsT_scale=w1_plane[:, a, s * P : (s + 1) * P],
+                        rhs=v_words[a][:, cols].bitcast(FP8X4),
+                        rhs_scale=v_plane[:, a, cols],
+                        start=(a == 0),
+                        stop=(a == PASSES1 - 1),
+                    )
+                nc.scalar.activation(h[:, cols], acc[:], ACT.Tanh)
+            return h, wg
+
+        def put_entries(s, h, wg):
+            if s == 0:
+                for half in range(2):
+                    cols = slice(half * BANK, (half + 1) * BANK)
+                    nc.vector.tensor_tensor(
+                        page[s][:].indirect(idx2[:, half * 32 : (half + 1) * 32]), h[:, cols], wg[:, cols], ALU.mult
+                    )
+            else:
+                nc.vector.tensor_tensor(page[s][:].indirect(idx2[:]), h[:], wg[:], ALU.mult)
+
+        def features(s):
+            b, c = divmod(s, PACK)
+            due = keep.tile([P, M], F32, name="due", bufs=3)
+            nc.vector.tensor_copy(due[:], page[s][:].indirect(idx3[:]))
+            x = keep.tile([P, M], BF16, name="x", bufs=4)
+            nc.scalar.activation(x[:], due[:], ACT.Square, scale=sc_sb[:, s : s + 1])
+            nc.scalar.dma_start(x_rows[b][32 * c : 32 * c + 32, :, :], x[:])
+
+        def quantise_x(b):
+            grouped = keep.tile([P, M * PACK], BF16, name=f"x_grouped{b}", tag=f"x_grouped{b}", align_bytes=64)
+            nc.scalar.copy(
+                grouped[:].rearrange("p (c i j) -> p c j i", i=4, j=PACK),
+                x_rows[b][:].rearrange("p j (c i) -> p c j i", i=4),
+            )
+            nc.vector.quantize_mx(x_codes[b][:].bitcast(FP8X4), x_plane[b][:], grouped[:])
+
+        entries = [new_entries(s) for s in range(AHEAD)]
+        for s in range(SLICES):
+            put_entries(s, *entries[s])
+            if s + AHEAD < SLICES:
+                entries.append(new_entries(s + AHEAD))
+            if s >= 1:
+                features(s - 1)
+            if s == PACK:
+                quantise_x(0)
+            if 2 <= s < 2 + PASSES2 * H // W2_CHUNK:
+                quantise_w2(s - 2)
+        features(SLICES - 1)
+        quantise_x(1)
+
+        twin_early = keep.tile([P, TWINS_EARLY, M], F32, name="twin_early", tag="big0", align_bytes=64)
+        twin_late = keep.tile(
+            [P, SLICES - TWINS_EARLY, M], F32, name="twin_late", tag=f"x_grouped{PASSES2 - 1}", align_bytes=64
+        )
+        twin = [twin_early[:, s, :] for s in range(TWINS_EARLY)]
+        twin = twin + [twin_late[:, s, :] for s in range(SLICES - TWINS_EARLY)]
+        for s in range(SLICES):
+            nc.vector.tensor_copy(twin[s], page[s][:].indirect(idx4[:]))
+
+        y = [psum.tile([P, BANK], F32, name="bank") for s in range(SLICES)]
+        for b in range(PASSES2):
+            for s in range(SLICES):
+                nc.tensor.matmul_mx(
+                    y[s][:],
+                    lhsT=w2_codes[:, b, s * P : (s + 1) * P].bitcast(FP8X4),
+                    lhsT_scale=w2_plane[:, b, s * P : (s + 1) * P],
+                    rhs=x_codes[b][:].bitcast(FP8X4),
+                    rhs_scale=x_plane[b][:],
+                    start=(b == 0),
+                    stop=(b == PASSES2 - 1),
+                )
+        for s in range(SLICES):
+            diff = keep.tile([P, M], F32, name="diff", bufs=3)
+            nc.vector.scalar_tensor_tensor(diff[:], twin[s], tw_sb[:, s : s + 1], y[s][:], ALU.mult, ALU.subtract)
+            res = keep.tile([P, M], F32, name="res", bufs=4)
+            nc.scalar.activation(res[:], diff[:], ACT.Abs)
+            nc.sync.dma_start(out[s * P : (s + 1) * P, :], res[:])

@@ -1,6 +1,7 @@
 from contextlib import ExitStack
 
 import concourse.mybir as mybir
+from concourse.masks import make_identity
 
 K, H, T, S, T2, M = 1536, 1024, 4096, 1024, 2048, 512
 FLOPS = 2 * K * H * S + 2 * H * H * M
@@ -44,22 +45,42 @@ def tile_list_die_wear_ledger_kernel(
 
         tab_sc = keep.tile([P, T], U8, name="tab_sc", align_bytes=64)
         v_plane = keep.tile([P, PASSES1, S], U8, name="v_plane", align_bytes=64)
-        w1_plane = keep.tile([P, PASSES1, H], U8, name="w1_plane", align_bytes=64)
-        nc.vector.memset(w1_plane[:].bitcast(I32), 0)
+        early_cols = P * W1_EARLY
+        w1_plane_early = keep.tile([P, PASSES1, early_cols], U8, name="w1_plane_early", align_bytes=64)
+        w1_plane_late = keep.tile([P, PASSES1, H - early_cols], U8, name="w1_plane_late", align_bytes=64)
+        gain_rows = keep.tile([P, P], F32, name="gain_rows")
+        factor_rows = keep.tile([P, P], F32, name="factor_rows")
+        identity = keep.tile([P, P], F32, name="identity")
+        nc.gpsimd.memset(w1_plane_early[:].bitcast(I32), 0)
+        nc.gpsimd.memset(gain_rows[:], 0.0)
+        make_identity(nc, identity[:])
+        nc.gpsimd.memset(factor_rows[:], 0.0)
         nc.vector.memset(tab_sc[0:16, :].bitcast(I32), 0)
         nc.vector.memset(tab_sc[64:128, :].bitcast(I32), 0)
         nc.vector.memset(v_plane[:].bitcast(I32), 0)
+        nc.vector.memset(w1_plane_late[:].bitcast(I32), 0)
 
         tab = [keep.tile([P, T], U32, name=f"tab{a}", tag=f"big{a}", align_bytes=64) for a in range(PASSES1)]
 
         def load_tab(a):
             nc.sync.dma_start(tab[a][:].bitcast(I32), tab_words[a].rearrange("p t i -> p (t i)").bitcast(I32))
 
-        def load_column_vector(queue, name, vec):
-            col = keep.tile([P, SLICES], F32, name=name)
-            with nc.allow_non_contiguous_dma(reason="one value a partition and slice"):
-                queue.dma_start(col[:], vec.rearrange("(s p) -> p s", p=P))
-            return col
+        def load_w1_plane(plane, c0, c1):
+            for q in range(4):
+                nc.sync.dma_start(
+                    plane[32 * q : 32 * q + 4, :, :].bitcast(I32),
+                    w1_scales[:, 4 * q : 4 * q + 4, c0:c1].rearrange("a r c -> r a c").bitcast(I32),
+                )
+
+        def load_rows(queue, rows, place, vec):
+            queue.dma_start(rows[place * SLICES : (place + 1) * SLICES, :], vec.rearrange("(s p) -> s p", p=P))
+
+        def turn_to_columns(name, rows, count):
+            turned = psum.tile([P, BANK], F32, name="bank")
+            nc.tensor.transpose(turned[:, 0:P], rows[:], identity[:])
+            cols = keep.tile([P, count], F32, name=name)
+            nc.scalar.copy(cols[:], turned[:, 0:count])
+            return cols
 
         w1_rows = w1_words.rearrange("a p c -> p a c")
         early_bytes = 2 * P * W1_EARLY
@@ -74,28 +95,28 @@ def tile_list_die_wear_ledger_kernel(
         nc.sync.dma_start(idx[:], offs)
         nc.sync.dma_start(tab_sc[16:64, :].bitcast(I32), tab_scales.rearrange("a q t -> q a t").bitcast(I32))
         load_tab(0)
-        for q in range(4):
-            nc.sync.dma_start(
-                w1_plane[32 * q : 32 * q + 4, :, :].bitcast(I32),
-                w1_scales[:, 4 * q : 4 * q + 4, :].rearrange("a r c -> r a c").bitcast(I32),
-            )
+        load_rows(nc.scalar, gain_rows, 0, gain)
+        load_w1_plane(w1_plane_early, 0, early_cols)
         load_tab(1)
+        nc.sync.dma_start(w1_early[:].bitcast(I32), w1_rows[:, :, 0:early_bytes].bitcast(I32))
         v_sc = keep.tile([P, S], U8, name="v_sc", align_bytes=64)
         nc.vector.tensor_copy(v_sc[:], tab_sc[:].indirect(idx[:]))
         for q in range(4):
             nc.sync.dma_start(
                 v_plane[32 * q : 32 * q + 4, :, :].bitcast(I32), v_sc[16 + 12 * q : 28 + 12 * q, :].bitcast(I32)
             )
-        gain_sb = load_column_vector(nc.scalar, "gain_sb", gain)
-        sc_sb = load_column_vector(nc.scalar, "sc_sb", sc)
-        nc.sync.dma_start(w1_early[:].bitcast(I32), w1_rows[:, :, 0:early_bytes].bitcast(I32))
-        nc.sync.dma_start(idx2[:], offs2)
+        gain_sb = turn_to_columns("gain_sb", gain_rows, SLICES)
         load_tab(2)
-        nc.sync.dma_start(wgs_sb[:], wgs)
+        nc.sync.dma_start(idx2[:], offs2)
+        nc.sync.dma_start(wgs_sb[:, 0:BANK], wgs[:, 0:BANK])
         load_page(0)
+        nc.sync.dma_start(wgs_sb[:, BANK:S], wgs[:, BANK:S])
         nc.sync.dma_start(idx3[:], offs3)
-        load_page(1)
+        load_rows(nc.sync, factor_rows, 0, sc)
+        load_rows(nc.sync, factor_rows, 1, tw)
         nc.sync.dma_start(w1_late[:].bitcast(I32), w1_rows[:, :, early_bytes : 2 * H].bitcast(I32))
+        load_w1_plane(w1_plane_late, early_cols, H)
+        load_page(1)
 
         v_words = [keep.tile([P, S], U32, name=f"v_words{a}", align_bytes=64) for a in range(PASSES1)]
         for a in range(PASSES1 - 1):
@@ -106,16 +127,19 @@ def tile_list_die_wear_ledger_kernel(
                 tab[PASSES1 - 1][:].indirect(idx[:, half * 32 : (half + 1) * 32]),
             )
 
-        w2_raw = []
-        for b in range(PASSES2):
-            load_page(2 + b)
+        def load_w2(b):
             raw = keep.tile([P, PACK, H], F32, name=f"w2_raw{b}", tag=f"big{b + 1}", align_bytes=64)
             nc.sync.dma_start(raw[:], w2[b * 512 : (b + 1) * 512, :].rearrange("(p j) n -> p j n", j=PACK))
-            w2_raw.append(raw)
-        for s in range(2 + PASSES2, SLICES):
+            return raw
+
+        load_page(2)
+        w2_raw = [load_w2(0)]
+        load_page(3)
+        load_page(4)
+        w2_raw.append(load_w2(1))
+        for s in range(5, SLICES):
             load_page(s)
         nc.sync.dma_start(idx4[:], offs4)
-        tw_sb = load_column_vector(nc.sync, "tw_sb", tw)
 
         w2_codes = keep.tile([P, PASSES2, H], U32, name="w2_codes", align_bytes=64)
         w2_plane = keep.tile([P, PASSES2, H], U8, name="w2_plane", align_bytes=64)
@@ -132,28 +156,33 @@ def tile_list_die_wear_ledger_kernel(
             )
 
         x_rows = [keep.tile([P, PACK, M], BF16, name=f"x_rows{b}") for b in range(PASSES2)]
-        x_codes = [keep.tile([P, M], U32, name=f"x_codes{b}", align_bytes=64) for b in range(PASSES2)]
+        x_codes = []
         x_plane = [keep.tile([P, M], U8, name=f"x_plane{b}", align_bytes=64) for b in range(PASSES2)]
 
         def new_entries(s):
             if s < W1_EARLY:
-                w1_sb, c0 = w1_early, 2 * P * s
+                w1_sb, w1_plane, c0 = w1_early, w1_plane_early, P * s
             else:
-                w1_sb, c0 = w1_late, 2 * P * (s - W1_EARLY)
+                w1_sb, w1_plane, c0 = w1_late, w1_plane_late, P * (s - W1_EARLY)
             if s == SLICES - 1:
                 h = keep.tile([P, S], F32, name="h_last", tag="big0", align_bytes=64)
+            elif s == PACK + 1:
+                h = keep.tile([P, S], F32, name="h_under_x_codes", tag="x_codes0", align_bytes=64)
             else:
                 h = keep.tile([P, S], F32, name="h", bufs=3)
             wg = keep.tile([P, S], F32, name="wg", bufs=3)
-            nc.scalar.activation(wg[:], wgs_sb[:], ACT.Copy, scale=gain_sb[:, s : s + 1])
+            if s > 0:
+                nc.scalar.activation(wg[:], wgs_sb[:], ACT.Copy, scale=gain_sb[:, s : s + 1])
             for half in range(2):
                 cols = slice(half * BANK, (half + 1) * BANK)
+                if s == 0:
+                    nc.scalar.activation(wg[:, cols], wgs_sb[:, cols], ACT.Copy, scale=gain_sb[:, s : s + 1])
                 acc = psum.tile([P, BANK], F32, name="bank")
                 for a in range(PASSES1):
                     nc.tensor.matmul_mx(
                         acc[:],
-                        lhsT=w1_sb[:, a, c0 : c0 + 2 * P].bitcast(FP4X4),
-                        lhsT_scale=w1_plane[:, a, s * P : (s + 1) * P],
+                        lhsT=w1_sb[:, a, 2 * c0 : 2 * (c0 + P)].bitcast(FP4X4),
+                        lhsT_scale=w1_plane[:, a, c0 : c0 + P],
                         rhs=v_words[a][:, cols].bitcast(FP8X4),
                         rhs_scale=v_plane[:, a, cols],
                         start=(a == 0),
@@ -172,12 +201,11 @@ def tile_list_die_wear_ledger_kernel(
             else:
                 nc.vector.tensor_tensor(page[s][:].indirect(idx2[:]), h[:], wg[:], ALU.mult)
 
-        def features(s):
+        def features(s, due):
             b, c = divmod(s, PACK)
-            due = keep.tile([P, M], F32, name="due", bufs=3)
-            nc.vector.tensor_copy(due[:], page[s][:].indirect(idx3[:]))
+            nc.vector.tensor_copy(due, page[s][:].indirect(idx3[:]))
             x = keep.tile([P, M], BF16, name="x", bufs=4)
-            nc.scalar.activation(x[:], due[:], ACT.Square, scale=sc_sb[:, s : s + 1])
+            nc.scalar.activation(x[:], due, ACT.Square, scale=sc_sb[:, s : s + 1])
             nc.scalar.dma_start(x_rows[b][32 * c : 32 * c + 32, :, :], x[:])
 
         def quantise_x(b):
@@ -186,20 +214,25 @@ def tile_list_die_wear_ledger_kernel(
                 grouped[:].rearrange("p (c i j) -> p c j i", i=4, j=PACK),
                 x_rows[b][:].rearrange("p j (c i) -> p c j i", i=4),
             )
-            nc.vector.quantize_mx(x_codes[b][:].bitcast(FP8X4), x_plane[b][:], grouped[:])
+            codes = keep.tile([P, M], U32, name=f"x_codes{b}", tag=f"x_codes{b}", align_bytes=64)
+            nc.vector.quantize_mx(codes[:].bitcast(FP8X4), x_plane[b][:], grouped[:])
+            x_codes.append(codes)
 
         entries = [new_entries(s) for s in range(AHEAD)]
+        factors = turn_to_columns("factors", factor_rows, 2 * SLICES)
+        sc_sb, tw_sb = factors[:, 0:SLICES], factors[:, SLICES : 2 * SLICES]
         for s in range(SLICES):
             put_entries(s, *entries[s])
             if s + AHEAD < SLICES:
                 entries.append(new_entries(s + AHEAD))
             if s >= 1:
-                features(s - 1)
-            if s == PACK:
+                features(s - 1, entries[s][1][:, 0:M])
+            if s == PACK + 1:
                 quantise_x(0)
             if 2 <= s < 2 + PASSES2 * H // W2_CHUNK:
                 quantise_w2(s - 2)
-        features(SLICES - 1)
+        due_last = keep.tile([P, M], F32, name="due_last")
+        features(SLICES - 1, due_last[:])
         quantise_x(1)
 
         twin_early = keep.tile([P, TWINS_EARLY, M], F32, name="twin_early", tag="big0", align_bytes=64)

@@ -256,9 +256,13 @@ def tile_list_die_wear_ledger_kernel(
                     start=(b == 0),
                     stop=(b == PASSES2 - 1),
                 )
-        for s in range(SLICES):
-            diff = keep.tile([P, M], F32, name="diff", bufs=3)
-            nc.vector.scalar_tensor_tensor(diff[:], twin[s], tw_sb[:, s : s + 1], y[s][:], ALU.mult, ALU.subtract)
-            res = keep.tile([P, M], F32, name="res", bufs=4)
-            nc.scalar.activation(res[:], diff[:], ACT.Abs)
-            nc.sync.dma_start(out[s * P : (s + 1) * P, :], res[:])
+        diff = keep.tile([P, SLICES, M], F32, name="diff", tag="big1", align_bytes=64)
+        res = keep.tile([P, SLICES, M], F32, name="res", tag="big2", align_bytes=64)
+        pieces = [(s, slice(0, M)) for s in range(SLICES - 1)]
+        pieces = pieces + [(SLICES - 1, slice(0, M // 2)), (SLICES - 1, slice(M // 2, M))]
+        for s, cols in pieces:
+            nc.vector.scalar_tensor_tensor(
+                diff[:, s, cols], twin[s][:, cols], tw_sb[:, s : s + 1], y[s][:, cols], ALU.mult, ALU.subtract
+            )
+            nc.scalar.activation(res[:, s, cols], diff[:, s, cols], ACT.Abs)
+            nc.sync.dma_start(out[s * P : (s + 1) * P, cols], res[:, s, cols])

@@ -19,14 +19,19 @@ ALU = mybir.AluOpType
 
 P = 128
 PACK = 4
+QUADRANTS = 4
+PER_COLUMN = 16
 BANK = 512
 PASSES1 = K // (P * PACK)
 PASSES2 = H // (P * PACK)
 SLICES = H // P
+SCALE_ROWS = 4 * QUADRANTS * PASSES1
+SCALE_ROW0 = 64 - SCALE_ROWS
 W1_EARLY = 2
-TWINS_EARLY = 6
-W2_CHUNK = 512
 AHEAD = 2
+W2_CHUNK = 512
+W2_FIRST = 2
+TWINS_EARLY = 6
 
 
 def tile_list_die_wear_ledger_kernel(
@@ -38,10 +43,14 @@ def tile_list_die_wear_ledger_kernel(
         keep = ctx.enter_context(tc.tile_pool(name="keep", bufs=1))
         psum = ctx.enter_context(tc.psum_pool(name="psum", bufs=8))
 
-        idx = lists.tile([P, S // 16], U16, name="idx")
-        idx2 = lists.tile([P, S // 16], U16, name="idx2")
-        idx3 = lists.tile([P, M // 16], U16, name="idx3")
-        idx4 = lists.tile([P, M // 16], U16, name="idx4")
+        idx = lists.tile([P, S // PER_COLUMN], U16, name="idx")
+        idx2 = lists.tile([P, S // PER_COLUMN], U16, name="idx2")
+        idx3 = lists.tile([P, M // PER_COLUMN], U16, name="idx3")
+        idx4 = lists.tile([P, M // PER_COLUMN], U16, name="idx4")
+
+        def half_of(entries, half):
+            width = BANK // PER_COLUMN
+            return entries[:, half * width : (half + 1) * width]
 
         tab_sc = keep.tile([P, T], U8, name="tab_sc", align_bytes=64)
         v_plane = keep.tile([P, PASSES1, S], U8, name="v_plane", align_bytes=64)
@@ -55,8 +64,8 @@ def tile_list_die_wear_ledger_kernel(
         nc.gpsimd.memset(gain_rows[:], 0.0)
         make_identity(nc, identity[:])
         nc.gpsimd.memset(factor_rows[:], 0.0)
-        nc.vector.memset(tab_sc[0:16, :].bitcast(I32), 0)
-        nc.vector.memset(tab_sc[64:128, :].bitcast(I32), 0)
+        nc.vector.memset(tab_sc[0:SCALE_ROW0, :].bitcast(I32), 0)
+        nc.vector.memset(tab_sc[SCALE_ROW0 + SCALE_ROWS : P, :].bitcast(I32), 0)
         nc.vector.memset(v_plane[:].bitcast(I32), 0)
         nc.vector.memset(w1_plane_late[:].bitcast(I32), 0)
 
@@ -66,10 +75,10 @@ def tile_list_die_wear_ledger_kernel(
             nc.sync.dma_start(tab[a][:].bitcast(I32), tab_words[a].rearrange("p t i -> p (t i)").bitcast(I32))
 
         def load_w1_plane(plane, c0, c1):
-            for q in range(4):
+            for q in range(QUADRANTS):
                 nc.sync.dma_start(
                     plane[32 * q : 32 * q + 4, :, :].bitcast(I32),
-                    w1_scales[:, 4 * q : 4 * q + 4, c0:c1].rearrange("a r c -> r a c").bitcast(I32),
+                    w1_scales[:, 4 * q : 4 * q + 4, c0:c1].rearrange("a e c -> e a c").bitcast(I32),
                 )
 
         def load_rows(queue, rows, place, vec):
@@ -78,12 +87,12 @@ def tile_list_die_wear_ledger_kernel(
         def turn_to_columns(name, rows, count):
             turned = psum.tile([P, BANK], F32, name="bank")
             nc.tensor.transpose(turned[:, 0:P], rows[:], identity[:])
-            cols = keep.tile([P, count], F32, name=name)
-            nc.scalar.copy(cols[:], turned[:, 0:count])
-            return cols
+            columns = keep.tile([P, count], F32, name=name)
+            nc.scalar.copy(columns[:], turned[:, 0:count])
+            return columns
 
         w1_rows = w1_words.rearrange("a p c -> p a c")
-        early_bytes = 2 * P * W1_EARLY
+        early_bytes = 2 * early_cols
         w1_early = keep.tile([P, PASSES1, early_bytes], U8, name="w1_early", align_bytes=64)
         w1_late = keep.tile([P, PASSES1, 2 * H - early_bytes], U8, name="w1_late", align_bytes=64)
         wgs_sb = keep.tile([P, S], F32, name="wgs_sb")
@@ -93,18 +102,23 @@ def tile_list_die_wear_ledger_kernel(
             nc.sync.dma_start(page[s][:], page0[s * P : (s + 1) * P, :])
 
         nc.sync.dma_start(idx[:], offs)
-        nc.sync.dma_start(tab_sc[16:64, :].bitcast(I32), tab_scales.rearrange("a q t -> q a t").bitcast(I32))
+        nc.sync.dma_start(
+            tab_sc[SCALE_ROW0 : SCALE_ROW0 + SCALE_ROWS, :].bitcast(I32),
+            tab_scales.rearrange("a blk t -> blk a t").bitcast(I32),
+        )
         load_tab(0)
-        load_rows(nc.scalar, gain_rows, 0, gain)
         load_w1_plane(w1_plane_early, 0, early_cols)
         load_tab(1)
-        nc.sync.dma_start(w1_early[:].bitcast(I32), w1_rows[:, :, 0:early_bytes].bitcast(I32))
         v_sc = keep.tile([P, S], U8, name="v_sc", align_bytes=64)
         nc.vector.tensor_copy(v_sc[:], tab_sc[:].indirect(idx[:]))
-        for q in range(4):
+        per_quadrant = SCALE_ROWS // QUADRANTS
+        for q in range(QUADRANTS):
+            row0 = SCALE_ROW0 + per_quadrant * q
             nc.sync.dma_start(
-                v_plane[32 * q : 32 * q + 4, :, :].bitcast(I32), v_sc[16 + 12 * q : 28 + 12 * q, :].bitcast(I32)
+                v_plane[32 * q : 32 * q + 4, :, :].bitcast(I32), v_sc[row0 : row0 + per_quadrant, :].bitcast(I32)
             )
+        nc.sync.dma_start(w1_early[:].bitcast(I32), w1_rows[:, :, 0:early_bytes].bitcast(I32))
+        load_rows(nc.sync, gain_rows, 0, gain)
         gain_sb = turn_to_columns("gain_sb", gain_rows, SLICES)
         load_tab(2)
         nc.sync.dma_start(idx2[:], offs2)
@@ -124,12 +138,12 @@ def tile_list_die_wear_ledger_kernel(
         for half in range(2):
             nc.vector.tensor_copy(
                 v_words[PASSES1 - 1][:, half * BANK : (half + 1) * BANK],
-                tab[PASSES1 - 1][:].indirect(idx[:, half * 32 : (half + 1) * 32]),
+                tab[PASSES1 - 1][:].indirect(half_of(idx, half)),
             )
 
         def load_w2(b):
             raw = keep.tile([P, PACK, H], F32, name=f"w2_raw{b}", tag=f"big{b + 1}", align_bytes=64)
-            nc.sync.dma_start(raw[:], w2[b * 512 : (b + 1) * 512, :].rearrange("(p j) n -> p j n", j=PACK))
+            nc.sync.dma_start(raw[:], w2[b * P * PACK : (b + 1) * P * PACK, :].rearrange("(p j) n -> p j n", j=PACK))
             return raw
 
         load_page(2)
@@ -141,16 +155,19 @@ def tile_list_die_wear_ledger_kernel(
             load_page(s)
         nc.sync.dma_start(idx4[:], offs4)
 
+        def interleave(grouped, rows):
+            nc.scalar.copy(
+                grouped.rearrange("p (c i j) -> p c j i", i=4, j=PACK),
+                rows.rearrange("p j (c i) -> p c j i", i=4),
+            )
+
         w2_codes = keep.tile([P, PASSES2, H], U32, name="w2_codes", align_bytes=64)
         w2_plane = keep.tile([P, PASSES2, H], U8, name="w2_plane", align_bytes=64)
 
         def quantise_w2(chunk):
             b, c0 = divmod(chunk * W2_CHUNK, H)
             grouped = keep.tile([P, W2_CHUNK * PACK], BF16, name="w2_grouped", bufs=2, align_bytes=64)
-            nc.scalar.copy(
-                grouped[:].rearrange("p (c i j) -> p c j i", i=4, j=PACK),
-                w2_raw[b][:, :, c0 : c0 + W2_CHUNK].rearrange("p j (c i) -> p c j i", i=4),
-            )
+            interleave(grouped[:], w2_raw[b][:, :, c0 : c0 + W2_CHUNK])
             nc.vector.quantize_mx(
                 w2_codes[:, b, c0 : c0 + W2_CHUNK].bitcast(FP8X4), w2_plane[:, b, c0 : c0 + W2_CHUNK], grouped[:]
             )
@@ -158,6 +175,7 @@ def tile_list_die_wear_ledger_kernel(
         x_rows = [keep.tile([P, PACK, M], BF16, name=f"x_rows{b}") for b in range(PASSES2)]
         x_codes = []
         x_plane = [keep.tile([P, M], U8, name=f"x_plane{b}", align_bytes=64) for b in range(PASSES2)]
+        x0_after = PACK + 1
 
         def new_entries(s):
             if s < W1_EARLY:
@@ -166,11 +184,11 @@ def tile_list_die_wear_ledger_kernel(
                 w1_sb, w1_plane, c0 = w1_late, w1_plane_late, P * (s - W1_EARLY)
             if s == SLICES - 1:
                 h = keep.tile([P, S], F32, name="h_last", tag="big0", align_bytes=64)
-            elif s == PACK + 1:
+            elif s == x0_after:
                 h = keep.tile([P, S], F32, name="h_under_x_codes", tag="x_codes0", align_bytes=64)
             else:
-                h = keep.tile([P, S], F32, name="h", bufs=3)
-            wg = keep.tile([P, S], F32, name="wg", bufs=3)
+                h = keep.tile([P, S], F32, name="h", bufs=AHEAD + 1)
+            wg = keep.tile([P, S], F32, name="wg", bufs=AHEAD + 1)
             if s > 0:
                 nc.scalar.activation(wg[:], wgs_sb[:], ACT.Copy, scale=gain_sb[:, s : s + 1])
             for half in range(2):
@@ -195,25 +213,20 @@ def tile_list_die_wear_ledger_kernel(
             if s == 0:
                 for half in range(2):
                     cols = slice(half * BANK, (half + 1) * BANK)
-                    nc.vector.tensor_tensor(
-                        page[s][:].indirect(idx2[:, half * 32 : (half + 1) * 32]), h[:, cols], wg[:, cols], ALU.mult
-                    )
+                    nc.vector.tensor_tensor(page[s][:].indirect(half_of(idx2, half)), h[:, cols], wg[:, cols], ALU.mult)
             else:
                 nc.vector.tensor_tensor(page[s][:].indirect(idx2[:]), h[:], wg[:], ALU.mult)
 
         def features(s, due):
             b, c = divmod(s, PACK)
             nc.vector.tensor_copy(due, page[s][:].indirect(idx3[:]))
-            x = keep.tile([P, M], BF16, name="x", bufs=4)
+            x = keep.tile([P, M], BF16, name="x", bufs=PACK)
             nc.scalar.activation(x[:], due, ACT.Square, scale=sc_sb[:, s : s + 1])
             nc.scalar.dma_start(x_rows[b][32 * c : 32 * c + 32, :, :], x[:])
 
         def quantise_x(b):
             grouped = keep.tile([P, M * PACK], BF16, name=f"x_grouped{b}", tag=f"x_grouped{b}", align_bytes=64)
-            nc.scalar.copy(
-                grouped[:].rearrange("p (c i j) -> p c j i", i=4, j=PACK),
-                x_rows[b][:].rearrange("p j (c i) -> p c j i", i=4),
-            )
+            interleave(grouped[:], x_rows[b][:])
             codes = keep.tile([P, M], U32, name=f"x_codes{b}", tag=f"x_codes{b}", align_bytes=64)
             nc.vector.quantize_mx(codes[:].bitcast(FP8X4), x_plane[b][:], grouped[:])
             x_codes.append(codes)
@@ -222,18 +235,19 @@ def tile_list_die_wear_ledger_kernel(
         factors = turn_to_columns("factors", factor_rows, 2 * SLICES)
         sc_sb, tw_sb = factors[:, 0:SLICES], factors[:, SLICES : 2 * SLICES]
         for s in range(SLICES):
-            put_entries(s, *entries[s])
+            h_s, wg_s = entries[s]
+            put_entries(s, h_s, wg_s)
             if s + AHEAD < SLICES:
                 entries.append(new_entries(s + AHEAD))
             if s >= 1:
-                features(s - 1, entries[s][1][:, 0:M])
-            if s == PACK + 1:
+                features(s - 1, wg_s[:, 0:M])
+            if s == x0_after:
                 quantise_x(0)
-            if 2 <= s < 2 + PASSES2 * H // W2_CHUNK:
-                quantise_w2(s - 2)
+            if W2_FIRST <= s < W2_FIRST + PASSES2 * H // W2_CHUNK:
+                quantise_w2(s - W2_FIRST)
         due_last = keep.tile([P, M], F32, name="due_last")
         features(SLICES - 1, due_last[:])
-        quantise_x(1)
+        quantise_x(PASSES2 - 1)
 
         twin_early = keep.tile([P, TWINS_EARLY, M], F32, name="twin_early", tag="big0", align_bytes=64)
         twin_late = keep.tile(
@@ -256,6 +270,7 @@ def tile_list_die_wear_ledger_kernel(
                     start=(b == 0),
                     stop=(b == PASSES2 - 1),
                 )
+
         diff = keep.tile([P, SLICES, M], F32, name="diff", tag="big1", align_bytes=64)
         res = keep.tile([P, SLICES, M], F32, name="res", tag="big2", align_bytes=64)
         pieces = [(s, slice(0, M)) for s in range(SLICES - 1)]

from contextlib import ExitStack

import concourse.mybir as mybir
from concourse.masks import make_identity

K, H, T, S, T2, M = 1536, 1024, 4096, 1024, 2048, 512
FLOPS = 2 * K * H * S + 2 * H * H * M

F32 = mybir.dt.float32
BF16 = mybir.dt.bfloat16
I32 = mybir.dt.int32
U32 = mybir.dt.uint32
U16 = mybir.dt.uint16
U8 = mybir.dt.uint8
FP8X4 = mybir.dt.float8_e4m3fn_x4
FP4X4 = mybir.dt.float4_e2m1fn_x4
ACT = mybir.ActivationFunctionType
ALU = mybir.AluOpType

P = 128
PACK = 4
QUADRANTS = 4
PER_COLUMN = 16
BANK = 512
PASSES1 = K // (P * PACK)
PASSES2 = H // (P * PACK)
SLICES = H // P
SCALE_ROWS = 4 * QUADRANTS * PASSES1
SCALE_ROW0 = 64 - SCALE_ROWS
W1_EARLY = 2
AHEAD = 2
W2_CHUNK = 512
W2_FIRST = 2
TWINS_EARLY = 6


def tile_list_die_wear_ledger_kernel(
    tc, tab_words, tab_scales, offs, w1_words, w1_scales, gain, page0, wgs, offs2, offs3, offs4, sc, w2, tw, out
):
    nc = tc.nc
    with ExitStack() as ctx:
        lists = ctx.enter_context(tc.tile_pool(name="lists", bufs=1))
        keep = ctx.enter_context(tc.tile_pool(name="keep", bufs=1))
        psum = ctx.enter_context(tc.psum_pool(name="psum", bufs=8))

        idx = lists.tile([P, S // PER_COLUMN], U16, name="idx")
        idx2 = lists.tile([P, S // PER_COLUMN], U16, name="idx2")
        idx3 = lists.tile([P, M // PER_COLUMN], U16, name="idx3")
        idx4 = lists.tile([P, M // PER_COLUMN], U16, name="idx4")

        def half_of(entries, half):
            width = BANK // PER_COLUMN
            return entries[:, half * width : (half + 1) * width]

        tab_sc = keep.tile([P, T], U8, name="tab_sc", align_bytes=64)
        v_plane = keep.tile([P, PASSES1, S], U8, name="v_plane", align_bytes=64)
        early_cols = P * W1_EARLY
        w1_plane_early = keep.tile([P, PASSES1, early_cols], U8, name="w1_plane_early", align_bytes=64)
        w1_plane_late = keep.tile([P, PASSES1, H - early_cols], U8, name="w1_plane_late", align_bytes=64)
        gain_rows = keep.tile([P, P], F32, name="gain_rows")
        factor_rows = keep.tile([P, P], F32, name="factor_rows")
        identity = keep.tile([P, P], F32, name="identity")
        nc.gpsimd.memset(w1_plane_early[:].bitcast(I32), 0)
        nc.gpsimd.memset(gain_rows[:], 0.0)
        make_identity(nc, identity[:])
        nc.gpsimd.memset(factor_rows[:], 0.0)
        nc.vector.memset(tab_sc[0:SCALE_ROW0, :].bitcast(I32), 0)
        nc.vector.memset(tab_sc[SCALE_ROW0 + SCALE_ROWS : P, :].bitcast(I32), 0)
        nc.vector.memset(v_plane[:].bitcast(I32), 0)
        nc.vector.memset(w1_plane_late[:].bitcast(I32), 0)

        tab = [keep.tile([P, T], U32, name=f"tab{a}", tag=f"big{a}", align_bytes=64) for a in range(PASSES1)]

        def load_tab(a):
            nc.sync.dma_start(tab[a][:].bitcast(I32), tab_words[a].rearrange("p t i -> p (t i)").bitcast(I32))

        def load_w1_plane(plane, c0, c1):
            for q in range(QUADRANTS):
                nc.sync.dma_start(
                    plane[32 * q : 32 * q + 4, :, :].bitcast(I32),
                    w1_scales[:, 4 * q : 4 * q + 4, c0:c1].rearrange("a e c -> e a c").bitcast(I32),
                )

        def load_rows(queue, rows, place, vec):
            queue.dma_start(rows[place * SLICES : (place + 1) * SLICES, :], vec.rearrange("(s p) -> s p", p=P))

        def turn_to_columns(name, rows, count):
            turned = psum.tile([P, BANK], F32, name="bank")
            nc.tensor.transpose(turned[:, 0:P], rows[:], identity[:])
            columns = keep.tile([P, count], F32, name=name)
            nc.scalar.copy(columns[:], turned[:, 0:count])
            return columns

        w1_rows = w1_words.rearrange("a p c -> p a c")
        early_bytes = 2 * early_cols
        w1_early = keep.tile([P, PASSES1, early_bytes], U8, name="w1_early", align_bytes=64)
        w1_late = keep.tile([P, PASSES1, 2 * H - early_bytes], U8, name="w1_late", align_bytes=64)
        wgs_sb = keep.tile([P, S], F32, name="wgs_sb")
        page = [keep.tile([P, T2], F32, name=f"page{s}") for s in range(SLICES)]

        def load_page(s):
            nc.sync.dma_start(page[s][:], page0[s * P : (s + 1) * P, :])

        nc.sync.dma_start(idx[:], offs)
        nc.sync.dma_start(
            tab_sc[SCALE_ROW0 : SCALE_ROW0 + SCALE_ROWS, :].bitcast(I32),
            tab_scales.rearrange("a blk t -> blk a t").bitcast(I32),
        )
        load_tab(0)
        load_w1_plane(w1_plane_early, 0, early_cols)
        load_tab(1)
        v_sc = keep.tile([P, S], U8, name="v_sc", align_bytes=64)
        nc.vector.tensor_copy(v_sc[:], tab_sc[:].indirect(idx[:]))
        per_quadrant = SCALE_ROWS // QUADRANTS
        for q in range(QUADRANTS):
            row0 = SCALE_ROW0 + per_quadrant * q
            nc.sync.dma_start(
                v_plane[32 * q : 32 * q + 4, :, :].bitcast(I32), v_sc[row0 : row0 + per_quadrant, :].bitcast(I32)
            )
        nc.sync.dma_start(w1_early[:].bitcast(I32), w1_rows[:, :, 0:early_bytes].bitcast(I32))
        load_rows(nc.sync, gain_rows, 0, gain)
        gain_sb = turn_to_columns("gain_sb", gain_rows, SLICES)
        load_tab(2)
        nc.sync.dma_start(idx2[:], offs2)
        nc.sync.dma_start(wgs_sb[:, 0:BANK], wgs[:, 0:BANK])
        load_page(0)
        nc.sync.dma_start(wgs_sb[:, BANK:S], wgs[:, BANK:S])
        nc.sync.dma_start(idx3[:], offs3)
        load_rows(nc.sync, factor_rows, 0, sc)
        load_rows(nc.sync, factor_rows, 1, tw)
        nc.sync.dma_start(w1_late[:].bitcast(I32), w1_rows[:, :, early_bytes : 2 * H].bitcast(I32))
        load_w1_plane(w1_plane_late, early_cols, H)
        load_page(1)

        v_words = [keep.tile([P, S], U32, name=f"v_words{a}", align_bytes=64) for a in range(PASSES1)]
        for a in range(PASSES1 - 1):
            nc.vector.tensor_copy(v_words[a][:], tab[a][:].indirect(idx[:]))
        for half in range(2):
            nc.vector.tensor_copy(
                v_words[PASSES1 - 1][:, half * BANK : (half + 1) * BANK],
                tab[PASSES1 - 1][:].indirect(half_of(idx, half)),
            )

        def load_w2(b):
            raw = keep.tile([P, PACK, H], F32, name=f"w2_raw{b}", tag=f"big{b + 1}", align_bytes=64)
            nc.sync.dma_start(raw[:], w2[b * P * PACK : (b + 1) * P * PACK, :].rearrange("(p j) n -> p j n", j=PACK))
            return raw

        load_page(2)
        w2_raw = [load_w2(0)]
        load_page(3)
        load_page(4)
        w2_raw.append(load_w2(1))
        for s in range(5, SLICES):
            load_page(s)
        nc.sync.dma_start(idx4[:], offs4)

        def interleave(grouped, rows):
            nc.scalar.copy(
                grouped.rearrange("p (c i j) -> p c j i", i=4, j=PACK),
                rows.rearrange("p j (c i) -> p c j i", i=4),
            )

        w2_codes = keep.tile([P, PASSES2, H], U32, name="w2_codes", align_bytes=64)
        w2_plane = keep.tile([P, PASSES2, H], U8, name="w2_plane", align_bytes=64)

        def quantise_w2(chunk):
            b, c0 = divmod(chunk * W2_CHUNK, H)
            grouped = keep.tile([P, W2_CHUNK * PACK], BF16, name="w2_grouped", bufs=2, align_bytes=64)
            interleave(grouped[:], w2_raw[b][:, :, c0 : c0 + W2_CHUNK])
            nc.vector.quantize_mx(
                w2_codes[:, b, c0 : c0 + W2_CHUNK].bitcast(FP8X4), w2_plane[:, b, c0 : c0 + W2_CHUNK], grouped[:]
            )

        x_rows = [keep.tile([P, PACK, M], BF16, name=f"x_rows{b}") for b in range(PASSES2)]
        x_codes = []
        x_plane = [keep.tile([P, M], U8, name=f"x_plane{b}", align_bytes=64) for b in range(PASSES2)]
        x0_after = PACK + 1

        def new_entries(s):
            if s < W1_EARLY:
                w1_sb, w1_plane, c0 = w1_early, w1_plane_early, P * s
            else:
                w1_sb, w1_plane, c0 = w1_late, w1_plane_late, P * (s - W1_EARLY)
            if s == SLICES - 1:
                h = keep.tile([P, S], F32, name="h_last", tag="big0", align_bytes=64)
            elif s == x0_after:
                h = keep.tile([P, S], F32, name="h_under_x_codes", tag="x_codes0", align_bytes=64)
            else:
                h = keep.tile([P, S], F32, name="h", bufs=AHEAD + 1)
            wg = keep.tile([P, S], F32, name="wg", bufs=AHEAD + 1)
            if s > 0:
                nc.scalar.activation(wg[:], wgs_sb[:], ACT.Copy, scale=gain_sb[:, s : s + 1])
            for half in range(2):
                cols = slice(half * BANK, (half + 1) * BANK)
                if s == 0:
                    nc.scalar.activation(wg[:, cols], wgs_sb[:, cols], ACT.Copy, scale=gain_sb[:, s : s + 1])
                acc = psum.tile([P, BANK], F32, name="bank")
                for a in range(PASSES1):
                    nc.tensor.matmul_mx(
                        acc[:],
                        lhsT=w1_sb[:, a, 2 * c0 : 2 * (c0 + P)].bitcast(FP4X4),
                        lhsT_scale=w1_plane[:, a, c0 : c0 + P],
                        rhs=v_words[a][:, cols].bitcast(FP8X4),
                        rhs_scale=v_plane[:, a, cols],
                        start=(a == 0),
                        stop=(a == PASSES1 - 1),
                    )
                nc.scalar.activation(h[:, cols], acc[:], ACT.Tanh)
            return h, wg

        def put_entries(s, h, wg):
            if s == 0:
                for half in range(2):
                    cols = slice(half * BANK, (half + 1) * BANK)
                    nc.vector.tensor_tensor(page[s][:].indirect(half_of(idx2, half)), h[:, cols], wg[:, cols], ALU.mult)
            else:
                nc.vector.tensor_tensor(page[s][:].indirect(idx2[:]), h[:], wg[:], ALU.mult)

        def features(s, due):
            b, c = divmod(s, PACK)
            nc.vector.tensor_copy(due, page[s][:].indirect(idx3[:]))
            x = keep.tile([P, M], BF16, name="x", bufs=PACK)
            nc.scalar.activation(x[:], due, ACT.Square, scale=sc_sb[:, s : s + 1])
            nc.scalar.dma_start(x_rows[b][32 * c : 32 * c + 32, :, :], x[:])

        def quantise_x(b):
            grouped = keep.tile([P, M * PACK], BF16, name=f"x_grouped{b}", tag=f"x_grouped{b}", align_bytes=64)
            interleave(grouped[:], x_rows[b][:])
            codes = keep.tile([P, M], U32, name=f"x_codes{b}", tag=f"x_codes{b}", align_bytes=64)
            nc.vector.quantize_mx(codes[:].bitcast(FP8X4), x_plane[b][:], grouped[:])
            x_codes.append(codes)

        entries = [new_entries(s) for s in range(AHEAD)]
        factors = turn_to_columns("factors", factor_rows, 2 * SLICES)
        sc_sb, tw_sb = factors[:, 0:SLICES], factors[:, SLICES : 2 * SLICES]
        for s in range(SLICES):
            h_s, wg_s = entries[s]
            put_entries(s, h_s, wg_s)
            if s + AHEAD < SLICES:
                entries.append(new_entries(s + AHEAD))
            if s >= 1:
                features(s - 1, wg_s[:, 0:M])
            if s == x0_after:
                quantise_x(0)
            if W2_FIRST <= s < W2_FIRST + PASSES2 * H // W2_CHUNK:
                quantise_w2(s - W2_FIRST)
        due_last = keep.tile([P, M], F32, name="due_last")
        features(SLICES - 1, due_last[:])
        quantise_x(PASSES2 - 1)

        twin_early = keep.tile([P, TWINS_EARLY, M], F32, name="twin_early", tag="big0", align_bytes=64)
        twin_late = keep.tile(
            [P, SLICES - TWINS_EARLY, M], F32, name="twin_late", tag=f"x_grouped{PASSES2 - 1}", align_bytes=64
        )
        twin = [twin_early[:, s, :] for s in range(TWINS_EARLY)]
        twin = twin + [twin_late[:, s, :] for s in range(SLICES - TWINS_EARLY)]
        for s in range(SLICES):
            nc.vector.tensor_copy(twin[s], page[s][:].indirect(idx4[:]))

        y = [psum.tile([P, BANK], F32, name="bank") for s in range(SLICES)]
        for b in range(PASSES2):
            for s in range(SLICES):
                nc.tensor.matmul_mx(
                    y[s][:],
                    lhsT=w2_codes[:, b, s * P : (s + 1) * P].bitcast(FP8X4),
                    lhsT_scale=w2_plane[:, b, s * P : (s + 1) * P],
                    rhs=x_codes[b][:].bitcast(FP8X4),
                    rhs_scale=x_plane[b][:],
                    start=(b == 0),
                    stop=(b == PASSES2 - 1),
                )

        diff = keep.tile([P, SLICES, M], F32, name="diff", tag="big1", align_bytes=64)
        res = keep.tile([P, SLICES, M], F32, name="res", tag="big2", align_bytes=64)
        pieces = [(s, slice(0, M)) for s in range(SLICES - 1)]
        pieces = pieces + [(SLICES - 1, slice(0, M // 2)), (SLICES - 1, slice(M // 2, M))]
        for s, cols in pieces:
            nc.vector.scalar_tensor_tensor(
                diff[:, s, cols], twin[s][:, cols], tw_sb[:, s : s + 1], y[s][:, cols], ALU.mult, ALU.subtract
            )
            nc.scalar.activation(res[:, s, cols], diff[:, s, cols], ACT.Abs)
            nc.sync.dma_start(out[s * P : (s + 1) * P, cols], res[:, s, cols])
